import numpy as np
CORES = [113,118,241,246]
N = 4
W, KW, DIL = 128, 3, 8
H = (KW // 2) * DIL
def setup_inputs(rng):
    return {"x": rng.standard_normal((N, 128, W), dtype=np.float32), "w": rng.standard_normal((N, 128, KW * 128), dtype=np.float32)}
def setup_inputs_big(rng):
    d = setup_inputs(rng)
    for k in ("x", "w"): d[k] = (d[k].astype(np.float32) * 1024.0).astype(d[k].dtype)
    return d
def setup_inputs_small(rng):
    d = setup_inputs(rng)
    for k in ("x", "w"): d[k] = (d[k].astype(np.float32) * (1 / 1024.0)).astype(d[k].dtype)
    return d
def setup_inputs_apart(rng):
    d = setup_inputs(rng)
    f = (10.0 ** rng.permutation(np.linspace(-1.5, 1.5, N))).astype(np.float32).reshape(N, 1, 1)
    for k in ("x", "w"): d[k] = (d[k].astype(np.float32) * f).astype(d[k].dtype)
    return d
def reference(x, w):
    X, W_ = x.astype(np.float64), w.astype(np.float64)
    g = np.concatenate(list(X), axis=1)
    p = np.concatenate([g[:, -H:], g, g[:, :H]], axis=1)
    y = np.zeros((N, 128, W))
    for r in range(N):
        for i in range(KW):
            y[r] += W_[r][:, 128 * i:128 * i + 128].T @ p[:, W * r + i * DIL:W * r + i * DIL + W]
    return {"y": y.astype(np.float32 if x.dtype != np.float64 else np.float64)}

from concourse.bass import DstId, RemoteDMATransfer
from concourse.mybir import AluOpType

POS, TAPS, DIL = 128, 3, 8
HALO = (TAPS // 2) * DIL
NENG = 4

SCRATCH = {
    "xp": ("sbuf", [128, POS + 2 * HALO], "float32"),
    "ws": ("sbuf", [128, TAPS * 128], "float32"),
    "hl": ("sbuf", [128, HALO], "float32"),
    "hr": ("sbuf", [128, HALO], "float32"),
    "ys": ("sbuf", [128, POS], "float32"),
    "pa": ("psum", [128, 512], "float32"),
    "pl": ("psum", [128, 512], "float32"),
    "pr": ("psum", [128, 512], "float32"),
}
SEMAPHORES = ["xin", "win", "zero", "sent", "lin", "rin", "mma", "mml", "mmr", "cpy", "add", "out"]


def _bits(mask):
    return [b for b in range(mask.bit_length()) if (mask >> b) & 1]


def _spread(mask, n):
    bits = _bits(mask)
    picked = bits[::len(bits) // n][:n]
    return sum(1 << b for b in picked)


def rank_program(g, core, T, topo):
    r = T.rank_of(core)
    if r is None:
        return
    S = T.sem
    n = len(T.cores)
    left, right = T.cores[(r - 1) % n], T.cores[(r + 1) % n]

    g.sync.dma_start(T.xp[:, HALO:HALO + POS], T.x[:, :]).then_inc(S.xin, 16)
    g.scalar.dma_start(T.ws[:, :], T.w[:, :]).then_inc(S.win, 16)
    g.vector.memset(T.xp[:, 0:HALO], 0.0).then_inc(S.zero, 1)
    g.vector.memset(T.xp[:, HALO + POS:], 0.0).then_inc(S.zero, 1)

    sends = [
        (right, T.xp[:, POS:POS + HALO], T.hl[:, :], S.lin),
        (left, T.xp[:, HALO:2 * HALO], T.hr[:, :], S.rin),
    ]
    sends.sort(key=lambda s: len(_bits(topo.mask(core, s[0]))))
    used, seen, transfers = 0, 0, []
    for dst, src_ap, dst_ap, sem in sends:
        assert topo.may_write(core, dst)
        allowed = topo.mask(core, dst)
        free = allowed & ~seen
        if len(_bits(free)) < NENG:
            free = allowed & ~used
        m = _spread(free, NENG)
        used |= m
        seen |= allowed
        rid, pid = topo.addr(dst, core)
        transfers.append(RemoteDMATransfer(dst_ids=[DstId(rid=rid, pnc=pid)], dma_engine_mask=m,
                                           remote_sem=sem, src=src_ap, dst=dst_ap))
    g.wait_ge(S.xin, 16)
    g.remote_dma_fused(transfers, local_sem=S.sent)
    g.wait_ge(S.sent, NENG * len(transfers))

    te, ve = g.tensor, g.vector
    te.wait_ge(S.xin, 16)
    te.wait_ge(S.zero, 2)
    te.wait_ge(S.win, 16)
    for i in range(TAPS):
        mm = te.matmul(T.pa[:, 0:POS], T.ws[:, 128 * i:128 * i + 128], T.xp[:, DIL * i:DIL * i + POS],
                       start=(i == 0), stop=(i == TAPS - 1))
    mm.then_inc(S.mma, 1)
    ve.wait_ge(S.mma, 1)
    ve.tensor_copy(T.ys[:, :], T.pa[:, 0:POS]).then_inc(S.cpy, 1)
    ve.wait_ge(S.cpy, 1)

    edges = [
        (left, S.lin, 0, T.hl, T.pl, S.mml, 0),
        (right, S.rin, TAPS - 1, T.hr, T.pr, S.mmr, POS - HALO),
    ]
    edges.sort(key=lambda e: (topo.host(e[0]), topo.chip(e[0])) != (topo.host(core), topo.chip(core)))
    for _, arrived, tap, halo, bank, done, c0 in edges:
        te.wait_ge(arrived, NENG)
        te.matmul(bank[:, 0:HALO], T.ws[:, 128 * tap:128 * tap + 128], halo[:, :],
                  start=True, stop=True).then_inc(done, 1)
        ve.wait_ge(done, 1)
        ve.tensor_tensor(T.ys[:, c0:c0 + HALO], T.ys[:, c0:c0 + HALO], bank[:, 0:HALO],
                         AluOpType.add).then_inc(S.add, 1)

    g.sync.wait_ge(S.add, len(edges))
    g.sync.dma_start(T.y[:, :], T.ys[:, :]).then_inc(S.out, 16)
    g.sync.wait_ge(S.out, 16)
